import numpy as np
import ml_dtypes


def mxq(x, axis, fmt="e4m3"):
    dtype, down = {"e4m3": (ml_dtypes.float8_e4m3fn, 7), "e5m2": (ml_dtypes.float8_e5m2, 14)}[fmt]
    v = np.moveaxis(np.asarray(x, np.float32).astype(ml_dtypes.bfloat16).astype(np.float64), axis, -1)
    blocks = v.reshape(v.shape[:-1] + (-1, 32))
    amax = np.abs(blocks).max(-1, keepdims=True)
    byte = np.maximum(np.where(amax > 0, np.frexp(amax)[1] - 1 + 127, 0) - down, 1)
    scale = np.exp2(byte - 127.0)
    codes = (blocks / scale).astype(np.float32).astype(dtype).astype(np.float64)
    return np.moveaxis((codes * scale).reshape(v.shape), -1, axis)


WIDE = False


def mx_kscale(k):
    if not WIDE:
        return np.ones(k)
    levels = np.array([10, -10, 5, -5, 0])
    if k % 512:
        return np.exp2(np.random.permutation(np.resize(levels, k // 32))).repeat(32)
    a = np.empty((k // 512, 16))
    for p in range(k // 512):
        a[p, :8] = np.random.permutation(np.resize(levels, 8))
        for g in range(8):
            far = levels[np.abs(levels - a[p, g]) >= 10]
            a[p, g + 8] = far[np.random.randint(len(far))]
    return np.exp2(a.ravel()).repeat(32)


def f64(x):
    return np.asarray(x).astype(np.float64)


def striped(idx):
    return np.tile(idx.reshape(-1, 16).T, (8, 1)).astype(np.uint16)


def unstriped(offs):
    return offs[:16].T.reshape(-1).astype(np.int64)


E2M1 = np.array([0.0, 0.5, 1.0, 1.5, 2.0, 3.0, 4.0, 6.0, -0.0, -0.5, -1.0, -1.5, -2.0, -3.0, -4.0, -6.0])


def pack_weight(w, fmt):
    k, n = w.shape
    w = f64(np.asarray(w, np.float32).astype(ml_dtypes.bfloat16)).reshape(k // 32, 32, n)
    amax = np.abs(w).max(1)
    if fmt == "e4m3":
        byte = np.frexp(amax)[1] - 1 + 127 - 7
    else:
        mant, ex = np.frexp(amax / 6.0)
        byte = np.where(mant > 0.5, ex, ex - 1) + 127
    byte = np.clip(np.where(amax > 0, byte, 1), 1, 254)
    scaled = (w * np.exp2(127.0 - byte)[:, None, :]).reshape(k, n).astype(np.float32)
    by_word = np.ascontiguousarray(scaled.reshape(k // 512, 128, 4, n).transpose(0, 1, 3, 2))
    if fmt == "e4m3":
        words = by_word.astype(ml_dtypes.float8_e4m3fn).view(np.uint8)
    else:
        c = by_word.astype(ml_dtypes.float4_e2m1fn).view(np.uint8) & 0xF
        words = (c[..., 0::2] | (c[..., 1::2] << 4)).reshape(k // 512, 128, 2 * n)
    return np.ascontiguousarray(words), np.ascontiguousarray(byte.astype(np.uint8).reshape(k // 512, 16, n))


def unpack_weight(words, scales, fmt):
    g, _, n = scales.shape
    words = np.ascontiguousarray(words).reshape(g, 128, n, -1)
    if fmt == "e4m3":
        vals = words.view(ml_dtypes.float8_e4m3fn).astype(np.float64)
    else:
        nib = np.empty((g, 128, n, 4), np.uint8)
        nib[..., 0::2] = words & 0xF
        nib[..., 1::2] = words >> 4
        vals = E2M1[nib]
    vals = vals * np.repeat(np.exp2(scales.astype(np.float64) - 127.0), 8, axis=1)[..., None]
    return vals.transpose(0, 1, 3, 2).reshape(g * 512, n)


def pack_table(v):
    words, scales = pack_weight(v, "e4m3")
    return np.concatenate([words.reshape(words.shape[0], -1), scales.reshape(scales.shape[0], -1)], axis=1)


def unpack_table(tab):
    g, t = tab.shape[0], tab.shape[1] // 528
    return unpack_weight(tab[:, :512 * t].reshape(g, 128, t, 4), tab[:, 512 * t:].reshape(g, 16, t), "e4m3")


K, M, T, S = 1024, 1024, 2048, 256


def setup_inputs():
    n = np.random.standard_normal
    s = mx_kscale(K)[:, None]
    p_w0 = pack_weight(n((K, M)) / np.sqrt(3 * K) / s, "e2m1")
    p_w1 = pack_weight(n((K, M)) / np.sqrt(3 * K) / s, "e4m3")
    return {
        "tab": pack_table(n((K, T)) * s),
        "w0_words": p_w0[0],
        "w0_scales": p_w0[1],
        "w1_words": p_w1[0],
        "w1_scales": p_w1[1],
        "w2": (n((K, M)) / np.sqrt(3 * K) / s).astype(np.float32),
        "offs": striped(np.concatenate([np.random.permutation(T)[:S] for _ in range(3)])),
    }


def reference(tab, w0_words, w0_scales, w1_words, w1_scales, w2, offs):
    v = unpack_table(tab)
    idx = unstriped(offs).reshape(3, S)
    w0_ = unpack_weight(w0_words, w0_scales, "e2m1")
    w1_ = unpack_weight(w1_words, w1_scales, "e4m3")
    w2_ = mxq(f64(w2), 0, "e4m3")
    y = w0_.T @ v[:, idx[0]] + w1_.T @ v[:, idx[1]] + w2_.T @ v[:, idx[2]]
    return y

@@ -1,0 +1,152 @@
+from contextlib import ExitStack
+
+import concourse.mybir as mybir
+
+K, M, T, S = 1024, 1024, 2048, 256
+FLOPS = 2 * 3 * K * M * S
+
+F32 = mybir.dt.float32
+BF16 = mybir.dt.bfloat16
+I32 = mybir.dt.int32
+U32 = mybir.dt.uint32
+U16 = mybir.dt.uint16
+U8 = mybir.dt.uint8
+FP8X4 = mybir.dt.float8_e4m3fn_x4
+FP4X4 = mybir.dt.float4_e2m1fn_x4
+
+P = 128
+PASSES = 2
+PICKS = 3 * S
+N_TILES = M // P
+PIECE = 256
+CHUNK = 512
+
+
+def tile_list_tabfield_none_kernel(tc, tab, w0_words, w0_scales, w1_words, w1_scales, w2, offs, out):
+    nc = tc.nc
+    with ExitStack() as ctx:
+        sb = ctx.enter_context(tc.tile_pool(name="sb", bufs=1))
+        psum = ctx.enter_context(tc.psum_pool(name="psum", bufs=1))
+
+        offsets = sb.tile([P, PICKS // 16], U16, name="offsets")
+        tab_words = [sb.tile([P, T], I32, name="tab_words%d" % a, align_bytes=64) for a in range(PASSES)]
+        tab_scales = sb.tile([P, PASSES, T], U8, name="tab_scales", align_bytes=64)
+        w0_sb = sb.tile([P, PASSES, 2 * M], U8, name="w0_sb", align_bytes=64)
+        w0_sc = sb.tile([P, PASSES, M], U8, name="w0_sc", align_bytes=64)
+        w1_sc = sb.tile([P, PASSES, M], U8, name="w1_sc", align_bytes=64)
+        W1_OFF = 8
+
+        nc.vector.memset(tab_scales[:].bitcast(I32), 0)
+        nc.vector.memset(w0_sc[:].bitcast(I32), 0)
+        nc.vector.memset(w1_sc[:].bitcast(I32), 0)
+
+        def load_scale_rows(queue, plane, rows, first):
+            by_row = rows.rearrange("a (q r) n -> r q a n", r=4)
+            for r in range(4):
+                queue.dma_start(out=plane[:].bitcast(I32)[first + r : P : 32, :, :], in_=by_row[r].bitcast(I32))
+
+        def load_tab_words(a):
+            nc.sync.dma_start(out=tab_words[a][:], in_=tab[a, 0 : 4 * P * T].rearrange("(p t) -> p t", p=P).bitcast(I32))
+
+        w2_raw = {}
+
+        def load_w2(a, h):
+            raw = sb.tile([P, 4, CHUNK], F32, name="w2_raw%d%d" % (a, h), align_bytes=64)
+            rows = w2[512 * a : 512 * (a + 1), CHUNK * h : CHUNK * (h + 1)]
+            nc.sync.dma_start(out=raw[:], in_=rows.rearrange("(p i) n -> p i n", i=4))
+            w2_raw[a, h] = raw
+
+        w1_sb = []
+
+        def load_w1(q):
+            words = sb.tile([P, PASSES, PIECE], I32, name="w1_sb%d" % q, align_bytes=64)
+            src = w1_words.rearrange("a p n i -> p a (n i)")[:, :, 4 * PIECE * q : 4 * PIECE * (q + 1)]
+            nc.sync.dma_start(out=words[:], in_=src.bitcast(I32))
+            w1_sb.append(words)
+
+        tab_rows = tab[:, 4 * P * T :].rearrange("a (q t) -> a q t", q=16)
+        nc.sync.dma_start(offsets[:], offs)
+        load_tab_words(0)
+        load_scale_rows(nc.gpsimd, tab_scales, tab_rows, 0)
+        load_tab_words(1)
+        nc.sync.dma_start(out=w0_sb[:].bitcast(I32), in_=w0_words.rearrange("a p n -> p a n").bitcast(I32))
+        load_scale_rows(nc.sync, w0_sc, w0_scales, 0)
+        load_w2(0, 0)
+        load_w2(1, 0)
+        load_scale_rows(nc.sync, w1_sc, w1_scales, W1_OFF)
+        load_w2(0, 1)
+        load_w2(1, 1)
+        for q in range(M // PIECE):
+            load_w1(q)
+
+        got_words = [sb.tile([P, PICKS], U32, name="got_words%d" % a, align_bytes=64) for a in range(PASSES)]
+        got_scales = [sb.tile([P, PICKS], U8, name="got_scales%d" % a, align_bytes=64) for a in range(PASSES)]
+        for a in range(PASSES):
+            nc.vector.tensor_copy(got_words[a][:], tab_words[a][:].bitcast(U32).indirect(offsets[:]))
+            nc.vector.tensor_copy(got_scales[a][:], tab_scales[:, a, :].indirect(offsets[:]))
+
+        acc = [psum.tile([P, 512], F32, name="acc%d" % t) for t in range(N_TILES)]
+
+        def product(t, a, field, lhsT, lhsT_scale, cols, start=False, stop=False):
+            picks = slice(field * S + cols.start, field * S + cols.stop)
+            nc.tensor.matmul_mx(
+                out=acc[t][:, cols],
+                lhsT=lhsT,
+                lhsT_scale=lhsT_scale,
+                rhs=got_words[a][:, picks].bitcast(FP8X4),
+                rhs_scale=got_scales[a][:, picks],
+                start=start,
+                stop=stop,
+            )
+
+        for a in range(PASSES):
+            for t in range(N_TILES):
+                for half in range(2):
+                    product(
+                        t, a, 0,
+                        w0_sb[:, a, 2 * P * t : 2 * P * (t + 1)].bitcast(FP4X4),
+                        w0_sc[:, a, P * t : P * (t + 1)],
+                        slice(P * half, P * (half + 1)),
+                        start=(a == 0 and half == 0),
+                    )
+
+        on_vector = ((0, 1, 0), (1, 1, 0))
+        for h in range(M // CHUNK):
+            for a in range(PASSES):
+                grouped = []
+                for u in range(CHUNK // PIECE):
+                    g = sb.tile([P, PIECE, 4], BF16, name="grouped%d%d%d" % (a, h, u), align_bytes=64)
+                    dst = g[:].rearrange("p (c j) i -> p c i j", j=4)
+                    src = w2_raw[a, h][:, :, PIECE * u : PIECE * (u + 1)].rearrange("p i (c j) -> p c i j", j=4)
+                    if (a, h, u) in on_vector:
+                        nc.vector.tensor_copy(out=dst, in_=src)
+                    else:
+                        nc.scalar.copy(out=dst, in_=src)
+                    grouped.append(g)
+                for u in range(CHUNK // PIECE):
+                    codes = sb.tile([P, PIECE], U32, name="codes%d%d%d" % (a, h, u), align_bytes=64)
+                    scales = sb.tile([P, PIECE], U8, name="scales%d%d%d" % (a, h, u), align_bytes=64)
+                    nc.vector.quantize_mx(
+                        out=codes[:].bitcast(FP8X4), scales=scales[:], in_=grouped[u][:].rearrange("p c i -> p (c i)")
+                    )
+                    for s in range(PIECE // P):
+                        t = (CHUNK * h + PIECE * u) // P + s
+                        cols = slice(P * s, P * (s + 1))
+                        product(t, a, 2, codes[:, cols].bitcast(FP8X4), scales[:, cols], slice(0, S))
+
+        for t in range(N_TILES):
+            q, s = divmod(t, PIECE // P)
+            for a in range(PASSES):
+                product(
+                    t, a, 1,
+                    w1_sb[q][:, a, P * s : P * (s + 1)].bitcast(FP8X4),
+                    w1_sc[W1_OFF:P, a, P * t : P * (t + 1)],
+                    slice(0, S),
+                    stop=(a == PASSES - 1),
+                )
+            result = sb.tile([P, S], F32, name="result%d" % t, align_bytes=64)
+            if t % 2 == 0:
+                nc.vector.tensor_copy(out=result[:], in_=acc[t][:, 0:S])
+            else:
+                nc.scalar.copy(out=result[:], in_=acc[t][:, 0:S])
+            nc.sync.dma_start(out=out[P * t : P * (t + 1), :], in_=result[:])

@@ -31,7 +31,6 @@ def tile_list_tabfield_none_kernel(tc, tab, w0_words, w0_scales, w1_words, w1_sc
         offsets = sb.tile([P, PICKS // 16], U16, name="offsets")
         tab_words = [sb.tile([P, T], I32, name="tab_words%d" % a, align_bytes=64) for a in range(PASSES)]
         tab_scales = sb.tile([P, PASSES, T], U8, name="tab_scales", align_bytes=64)
-        w0_sb = sb.tile([P, PASSES, 2 * M], U8, name="w0_sb", align_bytes=64)
         w0_sc = sb.tile([P, PASSES, M], U8, name="w0_sc", align_bytes=64)
         w1_sc = sb.tile([P, PASSES, M], U8, name="w1_sc", align_bytes=64)
         W1_OFF = 8
@@ -50,34 +49,49 @@ def tile_list_tabfield_none_kernel(tc, tab, w0_words, w0_scales, w1_words, w1_sc
 
         w2_raw = {}
 
-        def load_w2(a, h):
-            raw = sb.tile([P, 4, CHUNK], F32, name="w2_raw%d%d" % (a, h), align_bytes=64)
-            rows = w2[512 * a : 512 * (a + 1), CHUNK * h : CHUNK * (h + 1)]
+        def load_w2(a, first, count):
+            raw = sb.tile([P, 4, P * count], F32, name="w2_raw%d%d" % (a, first), align_bytes=64)
+            rows = w2[512 * a : 512 * (a + 1), P * first : P * (first + count)]
             nc.sync.dma_start(out=raw[:], in_=rows.rearrange("(p i) n -> p i n", i=4))
-            w2_raw[a, h] = raw
+            for t in range(first, first + count):
+                w2_raw[a, t] = (raw, t - first)
 
-        w1_sb = []
+        w1_sb = {}
 
-        def load_w1(q):
-            words = sb.tile([P, PASSES, PIECE], I32, name="w1_sb%d" % q, align_bytes=64)
-            src = w1_words.rearrange("a p n i -> p a (n i)")[:, :, 4 * PIECE * q : 4 * PIECE * (q + 1)]
+        def load_w1(first, count):
+            words = sb.tile([P, PASSES, P * count], I32, name="w1_sb%d" % first, align_bytes=64)
+            src = w1_words.rearrange("a p n i -> p a (n i)")[:, :, 4 * P * first : 4 * P * (first + count)]
             nc.sync.dma_start(out=words[:], in_=src.bitcast(I32))
-            w1_sb.append(words)
+            for t in range(first, first + count):
+                w1_sb[t] = (words, t - first)
+
+        w0_sb = {}
+
+        def load_w0(first, count):
+            words = sb.tile([P, PASSES, 2 * P * count], U8, name="w0_sb%d" % first, align_bytes=64)
+            src = w0_words.rearrange("a p n -> p a n")[:, :, 2 * P * first : 2 * P * (first + count)]
+            nc.sync.dma_start(out=words[:].bitcast(I32), in_=src.bitcast(I32))
+            for t in range(first, first + count):
+                w0_sb[t] = (words, t - first)
 
         tab_rows = tab[:, 4 * P * T :].rearrange("a (q t) -> a q t", q=16)
-        nc.sync.dma_start(offsets[:], offs)
         load_tab_words(0)
-        load_scale_rows(nc.gpsimd, tab_scales, tab_rows, 0)
+        nc.sync.dma_start(offsets[:], offs)
+        load_scale_rows(nc.sync, tab_scales, tab_rows, 0)
         load_tab_words(1)
-        nc.sync.dma_start(out=w0_sb[:].bitcast(I32), in_=w0_words.rearrange("a p n -> p a n").bitcast(I32))
+        load_w0(0, 4)
         load_scale_rows(nc.sync, w0_sc, w0_scales, 0)
-        load_w2(0, 0)
-        load_w2(1, 0)
+        load_w2(0, 0, 4)
+        load_w2(1, 0, 4)
         load_scale_rows(nc.sync, w1_sc, w1_scales, W1_OFF)
-        load_w2(0, 1)
-        load_w2(1, 1)
-        for q in range(M // PIECE):
-            load_w1(q)
+        load_w1(0, 4)
+        load_w0(4, 4)
+        load_w2(0, 4, 4)
+        load_w2(1, 4, 2)
+        load_w2(1, 6, 2)
+        load_w1(4, 2)
+        load_w1(6, 1)
+        load_w1(7, 1)
 
         got_words = [sb.tile([P, PICKS], U32, name="got_words%d" % a, align_bytes=64) for a in range(PASSES)]
         got_scales = [sb.tile([P, PICKS], U8, name="got_scales%d" % a, align_bytes=64) for a in range(PASSES)]
@@ -99,54 +113,76 @@ def tile_list_tabfield_none_kernel(tc, tab, w0_words, w0_scales, w1_words, w1_sc
                 stop=stop,
             )
 
-        for a in range(PASSES):
-            for t in range(N_TILES):
-                for half in range(2):
-                    product(
-                        t, a, 0,
-                        w0_sb[:, a, 2 * P * t : 2 * P * (t + 1)].bitcast(FP4X4),
-                        w0_sc[:, a, P * t : P * (t + 1)],
-                        slice(P * half, P * (half + 1)),
-                        start=(a == 0 and half == 0),
-                    )
-
-        on_vector = ((0, 1, 0), (1, 1, 0))
-        for h in range(M // CHUNK):
+        def multiply_w0(first, count):
             for a in range(PASSES):
-                grouped = []
-                for u in range(CHUNK // PIECE):
-                    g = sb.tile([P, PIECE, 4], BF16, name="grouped%d%d%d" % (a, h, u), align_bytes=64)
-                    dst = g[:].rearrange("p (c j) i -> p c i j", j=4)
-                    src = w2_raw[a, h][:, :, PIECE * u : PIECE * (u + 1)].rearrange("p i (c j) -> p c i j", j=4)
-                    if (a, h, u) in on_vector:
-                        nc.vector.tensor_copy(out=dst, in_=src)
-                    else:
-                        nc.scalar.copy(out=dst, in_=src)
-                    grouped.append(g)
-                for u in range(CHUNK // PIECE):
-                    codes = sb.tile([P, PIECE], U32, name="codes%d%d%d" % (a, h, u), align_bytes=64)
-                    scales = sb.tile([P, PIECE], U8, name="scales%d%d%d" % (a, h, u), align_bytes=64)
-                    nc.vector.quantize_mx(
-                        out=codes[:].bitcast(FP8X4), scales=scales[:], in_=grouped[u][:].rearrange("p c i -> p (c i)")
-                    )
-                    for s in range(PIECE // P):
-                        t = (CHUNK * h + PIECE * u) // P + s
-                        cols = slice(P * s, P * (s + 1))
-                        product(t, a, 2, codes[:, cols].bitcast(FP8X4), scales[:, cols], slice(0, S))
+                for t in range(first, first + count):
+                    words, at = w0_sb[t]
+                    for half in range(2):
+                        product(
+                            t, a, 0,
+                            words[:, a, 2 * P * at : 2 * P * (at + 1)].bitcast(FP4X4),
+                            w0_sc[:, a, P * t : P * (t + 1)],
+                            slice(P * half, P * (half + 1)),
+                            start=(a == 0 and half == 0),
+                        )
 
-        for t in range(N_TILES):
-            q, s = divmod(t, PIECE // P)
+        def round_w2(a, first, count, on_vector):
+            raw, at = w2_raw[a, first]
+            g = sb.tile([P, P * count, 4], BF16, name="grouped%d%d" % (a, first), align_bytes=64)
+            dst = g[:].rearrange("p (c j) i -> p c i j", j=4)
+            src = raw[:, :, P * at : P * (at + count)].rearrange("p i (c j) -> p c i j", j=4)
+            if on_vector:
+                nc.vector.tensor_copy(out=dst, in_=src)
+            else:
+                nc.scalar.copy(out=dst, in_=src)
+            return g
+
+        def multiply_w2(a, first, count, g):
+            codes = sb.tile([P, P * count], U32, name="codes%d%d" % (a, first), align_bytes=64)
+            scales = sb.tile([P, P * count], U8, name="scales%d%d" % (a, first), align_bytes=64)
+            nc.vector.quantize_mx(out=codes[:].bitcast(FP8X4), scales=scales[:], in_=g[:].rearrange("p c i -> p (c i)"))
+            for s in range(count):
+                cols = slice(P * s, P * (s + 1))
+                product(first + s, a, 2, codes[:, cols].bitcast(FP8X4), scales[:, cols], slice(0, S))
+
+        def w2_pair(a, first, count, first_on_vector):
+            left = round_w2(a, first, count, first_on_vector)
+            right = round_w2(a, first + count, count, False)
+            multiply_w2(a, first, count, left)
+            multiply_w2(a, first + count, count, right)
+
+        def multiply_w1(t):
+            words, at = w1_sb[t]
             for a in range(PASSES):
                 product(
                     t, a, 1,
-                    w1_sb[q][:, a, P * s : P * (s + 1)].bitcast(FP8X4),
+                    words[:, a, P * at : P * (at + 1)].bitcast(FP8X4),
                     w1_sc[W1_OFF:P, a, P * t : P * (t + 1)],
                     slice(0, S),
                     stop=(a == PASSES - 1),
                 )
-            result = sb.tile([P, S], F32, name="result%d" % t, align_bytes=64)
-            if t % 2 == 0:
-                nc.vector.tensor_copy(out=result[:], in_=acc[t][:, 0:S])
-            else:
-                nc.scalar.copy(out=result[:], in_=acc[t][:, 0:S])
-            nc.sync.dma_start(out=out[P * t : P * (t + 1), :], in_=result[:])
+
+        def finish(first, count):
+            result = sb.tile([P, count, S], F32, name="result%d" % first, align_bytes=64)
+            for t in range(first, first + count):
+                multiply_w1(t)
+                if t % 2 == 1:
+                    nc.vector.tensor_copy(out=result[:, t - first, :], in_=acc[t][:, 0:S])
+                else:
+                    nc.scalar.copy(out=result[:, t - first, :], in_=acc[t][:, 0:S])
+            rows = out[P * first : P * (first + count), :].rearrange("(t p) j -> p t j", p=P)
+            nc.sync.dma_start(out=rows, in_=result[:])
+
+        multiply_w0(0, 4)
+        w2_pair(0, 0, 2, False)
+        w2_pair(1, 0, 2, True)
+        finish(0, 2)
+        finish(2, 2)
+        multiply_w0(4, 4)
+        w2_pair(0, 4, 2, True)
+        w2_pair(1, 4, 1, True)
+        finish(4, 1)
+        finish(5, 1)
+        w2_pair(1, 6, 1, True)
+        finish(6, 1)
+        finish(7, 1)

@@ -36,13 +36,12 @@ def tile_list_tabfield_none_kernel(tc, tab, w0_words, w0_scales, w1_words, w1_sc
         W1_OFF = 8
 
         nc.vector.memset(tab_scales[:].bitcast(I32), 0)
-        nc.vector.memset(w0_sc[:].bitcast(I32), 0)
         nc.vector.memset(w1_sc[:].bitcast(I32), 0)
+        nc.gpsimd.memset(w0_sc[:].bitcast(I32), 0)
 
-        def load_scale_rows(queue, plane, rows, first):
+        def load_scale_row(queue, plane, rows, first, r):
             by_row = rows.rearrange("a (q r) n -> r q a n", r=4)
-            for r in range(4):
-                queue.dma_start(out=plane[:].bitcast(I32)[first + r : P : 32, :, :], in_=by_row[r].bitcast(I32))
+            queue.dma_start(out=plane[:].bitcast(I32)[first + r : P : 32, :, :], in_=by_row[r].bitcast(I32))
 
         def load_tab_words(a):
             nc.sync.dma_start(out=tab_words[a][:], in_=tab[a, 0 : 4 * P * T].rearrange("(p t) -> p t", p=P).bitcast(I32))
@@ -75,23 +74,28 @@ def tile_list_tabfield_none_kernel(tc, tab, w0_words, w0_scales, w1_words, w1_sc
                 w0_sb[t] = (words, t - first)
 
         tab_rows = tab[:, 4 * P * T :].rearrange("a (q t) -> a q t", q=16)
+        load_scale_row(nc.gpsimd, w0_sc, w0_scales, 0, 0)
+        load_scale_row(nc.gpsimd, w0_sc, w0_scales, 0, 1)
+        load_scale_row(nc.gpsimd, w0_sc, w0_scales, 0, 2)
+        load_scale_row(nc.gpsimd, w0_sc, w0_scales, 0, 3)
         load_tab_words(0)
         nc.sync.dma_start(offsets[:], offs)
-        load_scale_rows(nc.sync, tab_scales, tab_rows, 0)
+        load_scale_row(nc.sync, tab_scales, tab_rows, 0, 0)
+        load_scale_row(nc.sync, w1_sc, w1_scales, W1_OFF, 0)
+        load_scale_row(nc.sync, tab_scales, tab_rows, 0, 1)
+        load_scale_row(nc.sync, tab_scales, tab_rows, 0, 2)
+        load_scale_row(nc.sync, tab_scales, tab_rows, 0, 3)
         load_tab_words(1)
-        load_w0(0, 4)
-        load_scale_rows(nc.sync, w0_sc, w0_scales, 0)
-        load_w2(0, 0, 4)
+        load_scale_row(nc.sync, w1_sc, w1_scales, W1_OFF, 1)
+        load_scale_row(nc.sync, w1_sc, w1_scales, W1_OFF, 2)
+        load_scale_row(nc.sync, w1_sc, w1_scales, W1_OFF, 3)
+        load_w0(0, 8)
+        load_w2(0, 0, 8)
         load_w2(1, 0, 4)
-        load_scale_rows(nc.sync, w1_sc, w1_scales, W1_OFF)
-        load_w1(0, 4)
-        load_w0(4, 4)
-        load_w2(0, 4, 4)
+        load_w1(0, 6)
         load_w2(1, 4, 2)
         load_w2(1, 6, 2)
-        load_w1(4, 2)
-        load_w1(6, 1)
-        load_w1(7, 1)
+        load_w1(6, 2)
 
         got_words = [sb.tile([P, PICKS], U32, name="got_words%d" % a, align_bytes=64) for a in range(PASSES)]
         got_scales = [sb.tile([P, PICKS], U8, name="got_scales%d" % a, align_bytes=64) for a in range(PASSES)]
@@ -137,52 +141,57 @@ def tile_list_tabfield_none_kernel(tc, tab, w0_words, w0_scales, w1_words, w1_sc
                 nc.scalar.copy(out=dst, in_=src)
             return g
 
-        def multiply_w2(a, first, count, g):
+        def multiply_w2(a, first, count, g, stop=False):
             codes = sb.tile([P, P * count], U32, name="codes%d%d" % (a, first), align_bytes=64)
             scales = sb.tile([P, P * count], U8, name="scales%d%d" % (a, first), align_bytes=64)
             nc.vector.quantize_mx(out=codes[:].bitcast(FP8X4), scales=scales[:], in_=g[:].rearrange("p c i -> p (c i)"))
             for s in range(count):
                 cols = slice(P * s, P * (s + 1))
-                product(first + s, a, 2, codes[:, cols].bitcast(FP8X4), scales[:, cols], slice(0, S))
+                product(first + s, a, 2, codes[:, cols].bitcast(FP8X4), scales[:, cols], slice(0, S), stop=stop)
 
-        def w2_pair(a, first, count, first_on_vector):
+        def w2_pair(a, first, count, first_on_vector, second_on_vector=False, stop=False):
             left = round_w2(a, first, count, first_on_vector)
-            right = round_w2(a, first + count, count, False)
-            multiply_w2(a, first, count, left)
-            multiply_w2(a, first + count, count, right)
+            right = round_w2(a, first + count, count, second_on_vector)
+            multiply_w2(a, first, count, left, stop)
+            multiply_w2(a, first + count, count, right, stop)
 
-        def multiply_w1(t):
-            words, at = w1_sb[t]
-            for a in range(PASSES):
-                product(
-                    t, a, 1,
-                    words[:, a, P * at : P * (at + 1)].bitcast(FP8X4),
-                    w1_sc[W1_OFF:P, a, P * t : P * (t + 1)],
-                    slice(0, S),
-                    stop=(a == PASSES - 1),
-                )
+        def multiply_w1(first, count, stop=False):
+            for t in range(first, first + count):
+                words, at = w1_sb[t]
+                for a in range(PASSES):
+                    product(
+                        t, a, 1,
+                        words[:, a, P * at : P * (at + 1)].bitcast(FP8X4),
+                        w1_sc[W1_OFF:P, a, P * t : P * (t + 1)],
+                        slice(0, S),
+                        stop=(stop and a == PASSES - 1),
+                    )
 
         def finish(first, count):
             result = sb.tile([P, count, S], F32, name="result%d" % first, align_bytes=64)
             for t in range(first, first + count):
-                multiply_w1(t)
-                if t % 2 == 1:
+                if t == N_TILES - 1:
                     nc.vector.tensor_copy(out=result[:, t - first, :], in_=acc[t][:, 0:S])
                 else:
                     nc.scalar.copy(out=result[:, t - first, :], in_=acc[t][:, 0:S])
             rows = out[P * first : P * (first + count), :].rearrange("(t p) j -> p t j", p=P)
             nc.sync.dma_start(out=rows, in_=result[:])
 
-        multiply_w0(0, 4)
-        w2_pair(0, 0, 2, False)
-        w2_pair(1, 0, 2, True)
-        finish(0, 2)
-        finish(2, 2)
-        multiply_w0(4, 4)
+        multiply_w0(0, 8)
+        w2_pair(0, 0, 2, True)
         w2_pair(0, 4, 2, True)
-        w2_pair(1, 4, 1, True)
-        finish(4, 1)
-        finish(5, 1)
-        w2_pair(1, 6, 1, True)
+        w2_pair(1, 0, 2, True)
+        multiply_w1(0, 2, True)
+        finish(0, 2)
+        multiply_w1(2, 2, True)
+        finish(2, 2)
+        multiply_w1(4, 2)
+        w2_pair(1, 4, 1, True, True, True)
+        finish(4, 2)
+        last = [round_w2(1, t, 1, True) for t in range(6, 8)]
+        multiply_w1(6, 1)
+        multiply_w2(1, 6, 1, last[0], True)
+        multiply_w1(7, 1)
+        multiply_w2(1, 7, 1, last[1], True)
         finish(6, 1)
         finish(7, 1)

from contextlib import ExitStack

import concourse.mybir as mybir

K, M, T, S = 1024, 1024, 2048, 256
FLOPS = 2 * 3 * K * M * S

F32 = mybir.dt.float32
BF16 = mybir.dt.bfloat16
I32 = mybir.dt.int32
U32 = mybir.dt.uint32
U16 = mybir.dt.uint16
U8 = mybir.dt.uint8
FP8X4 = mybir.dt.float8_e4m3fn_x4
FP4X4 = mybir.dt.float4_e2m1fn_x4

P = 128
PASSES = 2
PICKS = 3 * S
N_TILES = M // P
PIECE = 256
CHUNK = 512


def tile_list_tabfield_none_kernel(tc, tab, w0_words, w0_scales, w1_words, w1_scales, w2, offs, out):
    nc = tc.nc
    with ExitStack() as ctx:
        sb = ctx.enter_context(tc.tile_pool(name="sb", bufs=1))
        psum = ctx.enter_context(tc.psum_pool(name="psum", bufs=1))

        offsets = sb.tile([P, PICKS // 16], U16, name="offsets")
        tab_words = [sb.tile([P, T], I32, name="tab_words%d" % a, align_bytes=64) for a in range(PASSES)]
        tab_scales = sb.tile([P, PASSES, T], U8, name="tab_scales", align_bytes=64)
        w0_sc = sb.tile([P, PASSES, M], U8, name="w0_sc", align_bytes=64)
        w1_sc = sb.tile([P, PASSES, M], U8, name="w1_sc", align_bytes=64)
        W1_OFF = 8

        nc.vector.memset(tab_scales[:].bitcast(I32), 0)
        nc.vector.memset(w1_sc[:].bitcast(I32), 0)
        nc.gpsimd.memset(w0_sc[:].bitcast(I32), 0)

        def load_scale_row(queue, plane, rows, first, r):
            by_row = rows.rearrange("a (q r) n -> r q a n", r=4)
            queue.dma_start(out=plane[:].bitcast(I32)[first + r : P : 32, :, :], in_=by_row[r].bitcast(I32))

        def load_tab_words(a):
            nc.sync.dma_start(out=tab_words[a][:], in_=tab[a, 0 : 4 * P * T].rearrange("(p t) -> p t", p=P).bitcast(I32))

        w2_raw = {}

        def load_w2(a, first, count):
            raw = sb.tile([P, 4, P * count], F32, name="w2_raw%d%d" % (a, first), align_bytes=64)
            rows = w2[512 * a : 512 * (a + 1), P * first : P * (first + count)]
            nc.sync.dma_start(out=raw[:], in_=rows.rearrange("(p i) n -> p i n", i=4))
            for t in range(first, first + count):
                w2_raw[a, t] = (raw, t - first)

        w1_sb = {}

        def load_w1(first, count):
            words = sb.tile([P, PASSES, P * count], I32, name="w1_sb%d" % first, align_bytes=64)
            src = w1_words.rearrange("a p n i -> p a (n i)")[:, :, 4 * P * first : 4 * P * (first + count)]
            nc.sync.dma_start(out=words[:], in_=src.bitcast(I32))
            for t in range(first, first + count):
                w1_sb[t] = (words, t - first)

        w0_sb = {}

        def load_w0(first, count):
            words = sb.tile([P, PASSES, 2 * P * count], U8, name="w0_sb%d" % first, align_bytes=64)
            src = w0_words.rearrange("a p n -> p a n")[:, :, 2 * P * first : 2 * P * (first + count)]
            nc.sync.dma_start(out=words[:].bitcast(I32), in_=src.bitcast(I32))
            for t in range(first, first + count):
                w0_sb[t] = (words, t - first)

        tab_rows = tab[:, 4 * P * T :].rearrange("a (q t) -> a q t", q=16)
        load_scale_row(nc.gpsimd, w0_sc, w0_scales, 0, 0)
        load_scale_row(nc.gpsimd, w0_sc, w0_scales, 0, 1)
        load_scale_row(nc.gpsimd, w0_sc, w0_scales, 0, 2)
        load_scale_row(nc.gpsimd, w0_sc, w0_scales, 0, 3)
        load_tab_words(0)
        nc.sync.dma_start(offsets[:], offs)
        load_scale_row(nc.sync, tab_scales, tab_rows, 0, 0)
        load_scale_row(nc.sync, w1_sc, w1_scales, W1_OFF, 0)
        load_scale_row(nc.sync, tab_scales, tab_rows, 0, 1)
        load_scale_row(nc.sync, tab_scales, tab_rows, 0, 2)
        load_scale_row(nc.sync, tab_scales, tab_rows, 0, 3)
        load_tab_words(1)
        load_scale_row(nc.sync, w1_sc, w1_scales, W1_OFF, 1)
        load_scale_row(nc.sync, w1_sc, w1_scales, W1_OFF, 2)
        load_scale_row(nc.sync, w1_sc, w1_scales, W1_OFF, 3)
        load_w0(0, 8)
        load_w2(0, 0, 8)
        load_w2(1, 0, 4)
        load_w1(0, 6)
        load_w2(1, 4, 2)
        load_w2(1, 6, 2)
        load_w1(6, 2)

        got_words = [sb.tile([P, PICKS], U32, name="got_words%d" % a, align_bytes=64) for a in range(PASSES)]
        got_scales = [sb.tile([P, PICKS], U8, name="got_scales%d" % a, align_bytes=64) for a in range(PASSES)]
        for a in range(PASSES):
            nc.vector.tensor_copy(got_words[a][:], tab_words[a][:].bitcast(U32).indirect(offsets[:]))
            nc.vector.tensor_copy(got_scales[a][:], tab_scales[:, a, :].indirect(offsets[:]))

        acc = [psum.tile([P, 512], F32, name="acc%d" % t) for t in range(N_TILES)]

        def product(t, a, field, lhsT, lhsT_scale, cols, start=False, stop=False):
            picks = slice(field * S + cols.start, field * S + cols.stop)
            nc.tensor.matmul_mx(
                out=acc[t][:, cols],
                lhsT=lhsT,
                lhsT_scale=lhsT_scale,
                rhs=got_words[a][:, picks].bitcast(FP8X4),
                rhs_scale=got_scales[a][:, picks],
                start=start,
                stop=stop,
            )

        def multiply_w0(first, count):
            for a in range(PASSES):
                for t in range(first, first + count):
                    words, at = w0_sb[t]
                    for half in range(2):
                        product(
                            t, a, 0,
                            words[:, a, 2 * P * at : 2 * P * (at + 1)].bitcast(FP4X4),
                            w0_sc[:, a, P * t : P * (t + 1)],
                            slice(P * half, P * (half + 1)),
                            start=(a == 0 and half == 0),
                        )

        def round_w2(a, first, count, on_vector):
            raw, at = w2_raw[a, first]
            g = sb.tile([P, P * count, 4], BF16, name="grouped%d%d" % (a, first), align_bytes=64)
            dst = g[:].rearrange("p (c j) i -> p c i j", j=4)
            src = raw[:, :, P * at : P * (at + count)].rearrange("p i (c j) -> p c i j", j=4)
            if on_vector:
                nc.vector.tensor_copy(out=dst, in_=src)
            else:
                nc.scalar.copy(out=dst, in_=src)
            return g

        def multiply_w2(a, first, count, g, stop=False):
            codes = sb.tile([P, P * count], U32, name="codes%d%d" % (a, first), align_bytes=64)
            scales = sb.tile([P, P * count], U8, name="scales%d%d" % (a, first), align_bytes=64)
            nc.vector.quantize_mx(out=codes[:].bitcast(FP8X4), scales=scales[:], in_=g[:].rearrange("p c i -> p (c i)"))
            for s in range(count):
                cols = slice(P * s, P * (s + 1))
                product(first + s, a, 2, codes[:, cols].bitcast(FP8X4), scales[:, cols], slice(0, S), stop=stop)

        def w2_pair(a, first, count, first_on_vector, second_on_vector=False, stop=False):
            left = round_w2(a, first, count, first_on_vector)
            right = round_w2(a, first + count, count, second_on_vector)
            multiply_w2(a, first, count, left, stop)
            multiply_w2(a, first + count, count, right, stop)

        def multiply_w1(first, count, stop=False):
            for t in range(first, first + count):
                words, at = w1_sb[t]
                for a in range(PASSES):
                    product(
                        t, a, 1,
                        words[:, a, P * at : P * (at + 1)].bitcast(FP8X4),
                        w1_sc[W1_OFF:P, a, P * t : P * (t + 1)],
                        slice(0, S),
                        stop=(stop and a == PASSES - 1),
                    )

        def finish(first, count):
            result = sb.tile([P, count, S], F32, name="result%d" % first, align_bytes=64)
            for t in range(first, first + count):
                if t == N_TILES - 1:
                    nc.vector.tensor_copy(out=result[:, t - first, :], in_=acc[t][:, 0:S])
                else:
                    nc.scalar.copy(out=result[:, t - first, :], in_=acc[t][:, 0:S])
            rows = out[P * first : P * (first + count), :].rearrange("(t p) j -> p t j", p=P)
            nc.sync.dma_start(out=rows, in_=result[:])

        multiply_w0(0, 8)
        w2_pair(0, 0, 2, True)
        w2_pair(0, 4, 2, True)
        w2_pair(1, 0, 2, True)
        multiply_w1(0, 2, True)
        finish(0, 2)
        multiply_w1(2, 2, True)
        finish(2, 2)
        multiply_w1(4, 2)
        w2_pair(1, 4, 1, True, True, True)
        finish(4, 2)
        last = [round_w2(1, t, 1, True) for t in range(6, 8)]
        multiply_w1(6, 1)
        multiply_w2(1, 6, 1, last[0], True)
        multiply_w1(7, 1)
        multiply_w2(1, 7, 1, last[1], True)
        finish(6, 1)
        finish(7, 1)
